import numpy as np
import ml_dtypes


def mxq(x, axis, fmt="e4m3"):
    dtype, down = {"e4m3": (ml_dtypes.float8_e4m3fn, 7), "e5m2": (ml_dtypes.float8_e5m2, 14)}[fmt]
    v = np.moveaxis(np.asarray(x, np.float32).astype(ml_dtypes.bfloat16).astype(np.float64), axis, -1)
    blocks = v.reshape(v.shape[:-1] + (-1, 32))
    amax = np.abs(blocks).max(-1, keepdims=True)
    byte = np.maximum(np.where(amax > 0, np.frexp(amax)[1] - 1 + 127, 0) - down, 1)
    scale = np.exp2(byte - 127.0)
    codes = (blocks / scale).astype(np.float32).astype(dtype).astype(np.float64)
    return np.moveaxis((codes * scale).reshape(v.shape), -1, axis)


WIDE = False


def mx_kscale(k):
    if not WIDE:
        return np.ones(k)
    levels = np.array([10, -10, 5, -5, 0])
    if k % 512:
        return np.exp2(np.random.permutation(np.resize(levels, k // 32))).repeat(32)
    a = np.empty((k // 512, 16))
    for p in range(k // 512):
        a[p, :8] = np.random.permutation(np.resize(levels, 8))
        for g in range(8):
            far = levels[np.abs(levels - a[p, g]) >= 10]
            a[p, g + 8] = far[np.random.randint(len(far))]
    return np.exp2(a.ravel()).repeat(32)


def f64(x):
    return np.asarray(x).astype(np.float64)


def striped(idx):
    return np.tile(np.asarray(idx).reshape(-1, 16).T, (8, 1)).astype(np.uint16)


def unstriped(offs):
    return offs[:16].T.reshape(-1).astype(np.int64)


E2M1 = np.array([0.0, 0.5, 1.0, 1.5, 2.0, 3.0, 4.0, 6.0, -0.0, -0.5, -1.0, -1.5, -2.0, -3.0, -4.0, -6.0])


def pack_weight(w, fmt):
    k, n = w.shape
    w = f64(np.asarray(w, np.float32).astype(ml_dtypes.bfloat16)).reshape(k // 32, 32, n)
    amax = np.abs(w).max(1)
    if fmt == "e4m3":
        byte = np.frexp(amax)[1] - 1 + 127 - 7
    else:
        mant, ex = np.frexp(amax / 6.0)
        byte = np.where(mant > 0.5, ex, ex - 1) + 127
    byte = np.clip(np.where(amax > 0, byte, 1), 1, 254)
    scaled = (w * np.exp2(127.0 - byte)[:, None, :]).reshape(k, n).astype(np.float32)
    by_word = np.ascontiguousarray(scaled.reshape(k // 512, 128, 4, n).transpose(0, 1, 3, 2))
    if fmt == "e4m3":
        words = by_word.astype(ml_dtypes.float8_e4m3fn).view(np.uint8)
    else:
        c = by_word.astype(ml_dtypes.float4_e2m1fn).view(np.uint8) & 0xF
        words = (c[..., 0::2] | (c[..., 1::2] << 4)).reshape(k // 512, 128, 2 * n)
    return np.ascontiguousarray(words), np.ascontiguousarray(byte.astype(np.uint8).reshape(k // 512, 16, n))


def unpack_weight(words, scales, fmt):
    g, _, n = scales.shape
    words = np.ascontiguousarray(words).reshape(g, 128, n, -1)
    if fmt == "e4m3":
        vals = words.view(ml_dtypes.float8_e4m3fn).astype(np.float64)
    else:
        nib = np.empty((g, 128, n, 4), np.uint8)
        nib[..., 0::2] = words & 0xF
        nib[..., 1::2] = words >> 4
        vals = E2M1[nib]
    vals = vals * np.repeat(np.exp2(scales.astype(np.float64) - 127.0), 8, axis=1)[..., None]
    return vals.transpose(0, 1, 3, 2).reshape(g * 512, n)


def bf(x):
    return np.asarray(x, np.float32).astype(ml_dtypes.bfloat16)


def planes(Y):
    r, m = Y.shape
    b = f64(bf(Y)).reshape(r // 32, 32, m)
    amax = np.abs(b).max(1)
    byte = np.clip(np.where(amax > 0, np.frexp(amax)[1] - 1 + 127 - 7, 1), 1, 254)
    codes = (b * np.exp2(127.0 - byte)[:, None, :]).reshape(r, m).astype(np.float32).astype(ml_dtypes.float8_e4m3fn).view(np.uint8)
    words = codes.reshape(r // 512, 128, 4, m).transpose(0, 1, 3, 2)
    return np.ascontiguousarray(words), np.ascontiguousarray(byte.astype(np.uint8).reshape(r // 512, 16, m))


C, T, I, D = 512, 2048, 512, 512


def setup_inputs():
    n = np.random.standard_normal
    idx = np.random.permutation(T)[:I]
    fc = mx_kscale(C)
    codep = pack_weight(n((C, T)) / fc[:, None], "e4m3")
    return {
        "code_words": codep[0],
        "code_scales": codep[1],
        "dec": (n((C, D)) * 1 / np.sqrt(C) * fc[:, None]).astype(np.float32),
        "keys": (n((D, T))).astype(np.float32),
        "offs": striped(idx),
    }


def reference(code_words, code_scales, dec, keys, offs):
    idx = unstriped(offs)
    codeu = unpack_weight(code_words, code_scales, "e4m3")
    decq = mxq(f64(dec), 0, "e4m3")
    codeidxg = codeu[:, idx]
    b = decq.T @ codeidxg
    y = f64(keys)[:, idx] - b
    words, scales = planes(y)
    return y, words, scales

@@ -1,0 +1,127 @@
+from contextlib import ExitStack
+
+import concourse.mybir as mybir
+
+C, T, I, D = 512, 2048, 512, 512
+FLOPS = 2 * C * D * I
+
+F32 = mybir.dt.float32
+BF16 = mybir.dt.bfloat16
+I32 = mybir.dt.int32
+U32 = mybir.dt.uint32
+U16 = mybir.dt.uint16
+U8 = mybir.dt.uint8
+FP8X4 = mybir.dt.float8_e4m3fn_x4
+SUB = mybir.AluOpType.subtract
+
+P = 128
+PACK = 4
+CHUNK = 128
+
+
+def tile_attend_residualcache_pl_kernel(tc, code_words, code_scales, dec, keys, offs, out_0, out_1, out_2):
+    nc = tc.nc
+    with ExitStack() as ctx:
+        keep = ctx.enter_context(tc.tile_pool(name="keep", bufs=1))
+        psum = ctx.enter_context(tc.psum_pool(name="psum", bufs=1))
+
+        offsets = keep.tile([P, I // 16], U16, name="offsets")
+        dec_raw = keep.tile([P, PACK * D], F32, name="dec_raw", tag="slot_a")
+        words = keep.tile([P, T], U32, name="words", tag="slot_b")
+        scales = keep.tile([P, T], U8, name="scales")
+
+        nc.vector.memset(scales[:].bitcast(I32), 0)
+        nc.sync.dma_start(out=dec_raw[:], in_=dec.rearrange("(p j) d -> p (j d)", j=PACK))
+        nc.sync.dma_start(offsets[:], offs)
+        for q in range(4):
+            nc.sync.dma_start(
+                out=scales[32 * q : 32 * q + 4, :].bitcast(I32),
+                in_=code_scales[0, 4 * q : 4 * q + 4, :].bitcast(I32),
+            )
+        nc.sync.dma_start(
+            out=words[:].bitcast(I32),
+            in_=code_words[0].rearrange("p n t -> p (n t)").bitcast(I32),
+        )
+        key_rows = keys.rearrange("(p t) n -> t p n", t=PACK)
+        key_planes = []
+        for t in range(2):
+            plane = keep.tile([P, T], F32, name="keys%d" % t)
+            nc.sync.dma_start(out=plane[:], in_=key_rows[t])
+            key_planes.append(plane)
+
+        dec_bf = keep.tile([P, D * PACK], BF16, name="dec_bf", align_bytes=64)
+        nc.scalar.copy(
+            out=dec_bf[:].rearrange("p (t m j) -> p m j t", t=PACK, j=PACK),
+            in_=dec_raw[:].rearrange("p (j m t) -> p m j t", j=PACK, t=PACK),
+        )
+        scales_g = keep.tile([P, I], U8, name="scales_g", align_bytes=64)
+        nc.vector.tensor_copy(scales_g[:], scales[:].indirect(offsets[:]))
+        words_g = keep.tile([P, I], U32, name="words_g", align_bytes=64)
+        nc.vector.tensor_copy(words_g[:], words[:].indirect(offsets[:]))
+        dec_codes = keep.tile([P, D], U32, name="dec_codes", align_bytes=64)
+        dec_scales = keep.tile([P, D], U8, name="dec_scales", align_bytes=64)
+        nc.vector.quantize_mx(out=dec_codes[:].bitcast(FP8X4), scales=dec_scales[:], in_=dec_bf[:])
+
+        for t, tag in ((2, "slot_a"), (3, "slot_b")):
+            plane = keep.tile([P, T], F32, name="keys%d" % t, tag=tag)
+            nc.sync.dma_start(out=plane[:], in_=key_rows[t])
+            key_planes.append(plane)
+
+        decoded = []
+        for t in range(PACK):
+            cols = slice(P * t, P * (t + 1))
+            acc = psum.tile([P, I], F32, name="acc%d" % t)
+            nc.tensor.matmul_mx(
+                out=acc[:],
+                lhsT=dec_codes[:, cols].bitcast(FP8X4),
+                lhsT_scale=dec_scales[:, cols],
+                rhs=words_g[:].bitcast(FP8X4),
+                rhs_scale=scales_g[:],
+                start=True,
+                stop=True,
+            )
+            b = keep.tile([P, I], F32, name="b%d" % t)
+            nc.scalar.copy(out=b[:], in_=acc[:])
+            decoded.append(b)
+
+        y_rows = out_0.rearrange("(p t) i -> p t i", t=PACK)
+        y01 = keep.tile([P, 2, I], F32, name="y01")
+        y23 = keep.tile([P, 2, I], F32, name="y23")
+        chunks = range(I // CHUNK)
+        y_bf = [keep.tile([P, CHUNK, PACK], BF16, name="y_bf%d" % k, align_bytes=64) for k in chunks]
+        y_codes = keep.tile([P, I], U32, name="y_codes", align_bytes=64)
+        y_scales = keep.tile([P, I], U8, name="y_scales", align_bytes=64)
+
+        for t in range(2):
+            nc.vector.tensor_tensor(y01[:, t, :], key_planes[t][:].indirect(offsets[:]), decoded[t][:], SUB)
+        nc.sync.dma_start(out=y_rows[:, 0:2, :], in_=y01[:])
+        for k in chunks:
+            cols = slice(CHUNK * k, CHUNK * (k + 1))
+            nc.scalar.copy(out=y_bf[k][:, :, 0:2], in_=y01[:, :, cols].rearrange("p t i -> p i t"))
+        nc.vector.tensor_tensor(y23[:, 0, :], key_planes[2][:].indirect(offsets[:]), decoded[2][:], SUB)
+        nc.sync.dma_start(out=y_rows[:, 2, :], in_=y23[:, 0, :])
+
+        for k in chunks:
+            cols = slice(CHUNK * k, CHUNK * (k + 1))
+            listed = offsets[:, CHUNK // 16 * k : CHUNK // 16 * (k + 1)]
+            nc.vector.tensor_tensor(y23[:, 1, cols], key_planes[3][:].indirect(listed), decoded[3][:, cols], SUB)
+            nc.scalar.copy(out=y_bf[k][:, :, 2:4], in_=y23[:, :, cols].rearrange("p t i -> p i t"))
+        nc.sync.dma_start(out=y_rows[:, 3, :], in_=y23[:, 1, :])
+
+        word_rows = out_1[0].rearrange("p n t -> p (n t)").bitcast(I32)
+        for k in chunks:
+            cols = slice(CHUNK * k, CHUNK * (k + 1))
+            nc.vector.quantize_mx(
+                out=y_codes[:, cols].bitcast(FP8X4),
+                scales=y_scales[:, cols],
+                in_=y_bf[k][:].rearrange("p i t -> p (i t)"),
+            )
+            if k % 2 == 1:
+                half = slice(CHUNK * (k - 1), CHUNK * (k + 1))
+                nc.sync.dma_start(out=word_rows[:, half], in_=y_codes[:, half].bitcast(I32))
+        for q in range(4):
+            queue = nc.scalar if q % 2 == 0 else nc.sync
+            queue.dma_start(
+                out=out_2[0, 4 * q : 4 * q + 4, :].bitcast(I32),
+                in_=y_scales[32 * q : 32 * q + 4, :].bitcast(I32),
+            )

@@ -17,6 +17,7 @@ SUB = mybir.AluOpType.subtract
 P = 128
 PACK = 4
 CHUNK = 128
+SCALAR_M = 40
 
 
 def tile_attend_residualcache_pl_kernel(tc, code_words, code_scales, dec, keys, offs, out_0, out_1, out_2):
@@ -33,10 +34,10 @@ def tile_attend_residualcache_pl_kernel(tc, code_words, code_scales, dec, keys, 
         nc.vector.memset(scales[:].bitcast(I32), 0)
         nc.sync.dma_start(out=dec_raw[:], in_=dec.rearrange("(p j) d -> p (j d)", j=PACK))
         nc.sync.dma_start(offsets[:], offs)
-        for q in range(4):
+        for r in range(4):
             nc.sync.dma_start(
-                out=scales[32 * q : 32 * q + 4, :].bitcast(I32),
-                in_=code_scales[0, 4 * q : 4 * q + 4, :].bitcast(I32),
+                out=scales[r:P:32, :].bitcast(I32),
+                in_=code_scales[0, r:16:4, :].bitcast(I32),
             )
         nc.sync.dma_start(
             out=words[:].bitcast(I32),
@@ -50,10 +51,10 @@ def tile_attend_residualcache_pl_kernel(tc, code_words, code_scales, dec, keys, 
             key_planes.append(plane)
 
         dec_bf = keep.tile([P, D * PACK], BF16, name="dec_bf", align_bytes=64)
-        nc.scalar.copy(
-            out=dec_bf[:].rearrange("p (t m j) -> p m j t", t=PACK, j=PACK),
-            in_=dec_raw[:].rearrange("p (j m t) -> p m j t", j=PACK, t=PACK),
-        )
+        dealt = dec_bf[:].rearrange("p (t m j) -> p m t j", t=PACK, j=PACK)
+        source = dec_raw[:].rearrange("p (j m t) -> p m t j", j=PACK, t=PACK)
+        nc.scalar.copy(out=dealt[:, :SCALAR_M], in_=source[:, :SCALAR_M])
+        nc.vector.tensor_copy(out=dealt[:, SCALAR_M:], in_=source[:, SCALAR_M:])
         scales_g = keep.tile([P, I], U8, name="scales_g", align_bytes=64)
         nc.vector.tensor_copy(scales_g[:], scales[:].indirect(offsets[:]))
         words_g = keep.tile([P, I], U32, name="words_g", align_bytes=64)

@@ -17,7 +17,7 @@ SUB = mybir.AluOpType.subtract
 P = 128
 PACK = 4
 CHUNK = 128
-SCALAR_M = 40
+SCALAR_M = 80
 
 
 def tile_attend_residualcache_pl_kernel(tc, code_words, code_scales, dec, keys, offs, out_0, out_1, out_2):
@@ -29,23 +29,19 @@ def tile_attend_residualcache_pl_kernel(tc, code_words, code_scales, dec, keys, 
         offsets = keep.tile([P, I // 16], U16, name="offsets")
         dec_raw = keep.tile([P, PACK * D], F32, name="dec_raw", tag="slot_a")
         words = keep.tile([P, T], U32, name="words", tag="slot_b")
-        scales = keep.tile([P, T], U8, name="scales")
+        scales = keep.tile([P, T], U8, name="scales", tag="slot_c")
 
         nc.vector.memset(scales[:].bitcast(I32), 0)
         nc.sync.dma_start(out=dec_raw[:], in_=dec.rearrange("(p j) d -> p (j d)", j=PACK))
         nc.sync.dma_start(offsets[:], offs)
-        for r in range(4):
-            nc.sync.dma_start(
-                out=scales[r:P:32, :].bitcast(I32),
-                in_=code_scales[0, r:16:4, :].bitcast(I32),
-            )
+        nc.sync.dma_start(out=scales[32:96:4, :].bitcast(I32), in_=code_scales[0].bitcast(I32))
         nc.sync.dma_start(
             out=words[:].bitcast(I32),
             in_=code_words[0].rearrange("p n t -> p (n t)").bitcast(I32),
         )
         key_rows = keys.rearrange("(p t) n -> t p n", t=PACK)
         key_planes = []
-        for t in range(2):
+        for t in range(1):
             plane = keep.tile([P, T], F32, name="keys%d" % t)
             nc.sync.dma_start(out=plane[:], in_=key_rows[t])
             key_planes.append(plane)
@@ -55,15 +51,22 @@ def tile_attend_residualcache_pl_kernel(tc, code_words, code_scales, dec, keys, 
         source = dec_raw[:].rearrange("p (j m t) -> p m t j", j=PACK, t=PACK)
         nc.scalar.copy(out=dealt[:, :SCALAR_M], in_=source[:, :SCALAR_M])
         nc.vector.tensor_copy(out=dealt[:, SCALAR_M:], in_=source[:, SCALAR_M:])
+        scales_s = keep.tile([P, I], U8, name="scales_s", align_bytes=64)
+        nc.vector.tensor_copy(scales_s[:], scales[:].indirect(offsets[:]))
         scales_g = keep.tile([P, I], U8, name="scales_g", align_bytes=64)
-        nc.vector.tensor_copy(scales_g[:], scales[:].indirect(offsets[:]))
+        nc.vector.memset(scales_g[:].bitcast(I32), 0)
+        for r in range(4):
+            nc.sync.dma_start(
+                out=scales_g[r:P:32, :].bitcast(I32),
+                in_=scales_s[32 + 4 * r : 96 : 16, :].bitcast(I32),
+            )
         words_g = keep.tile([P, I], U32, name="words_g", align_bytes=64)
         nc.vector.tensor_copy(words_g[:], words[:].indirect(offsets[:]))
         dec_codes = keep.tile([P, D], U32, name="dec_codes", align_bytes=64)
         dec_scales = keep.tile([P, D], U8, name="dec_scales", align_bytes=64)
         nc.vector.quantize_mx(out=dec_codes[:].bitcast(FP8X4), scales=dec_scales[:], in_=dec_bf[:])
 
-        for t, tag in ((2, "slot_a"), (3, "slot_b")):
+        for t, tag in ((1, "slot_c"), (2, "slot_a"), (3, "slot_b")):
             plane = keep.tile([P, T], F32, name="keys%d" % t, tag=tag)
             nc.sync.dma_start(out=plane[:], in_=key_rows[t])
             key_planes.append(plane)

@@ -103,7 +103,7 @@ def tile_attend_residualcache_pl_kernel(tc, code_words, code_scales, dec, keys, 
             cols = slice(CHUNK * k, CHUNK * (k + 1))
             nc.scalar.copy(out=y_bf[k][:, :, 0:2], in_=y01[:, :, cols].rearrange("p t i -> p i t"))
         nc.vector.tensor_tensor(y23[:, 0, :], key_planes[2][:].indirect(offsets[:]), decoded[2][:], SUB)
-        nc.sync.dma_start(out=y_rows[:, 2, :], in_=y23[:, 0, :])
+        nc.scalar.dma_start(out=y_rows[:, 2, :], in_=y23[:, 0, :])
 
         for k in chunks:
             cols = slice(CHUNK * k, CHUNK * (k + 1))
@@ -122,7 +122,8 @@ def tile_attend_residualcache_pl_kernel(tc, code_words, code_scales, dec, keys, 
             )
             if k % 2 == 1:
                 half = slice(CHUNK * (k - 1), CHUNK * (k + 1))
-                nc.sync.dma_start(out=word_rows[:, half], in_=y_codes[:, half].bitcast(I32))
+                queue = nc.scalar if k == 1 else nc.sync
+                queue.dma_start(out=word_rows[:, half], in_=y_codes[:, half].bitcast(I32))
         for q in range(4):
             queue = nc.scalar if q % 2 == 0 else nc.sync
             queue.dma_start(

@@ -89,41 +89,54 @@ def tile_attend_residualcache_pl_kernel(tc, code_words, code_scales, dec, keys, 
             decoded.append(b)
 
         y_rows = out_0.rearrange("(p t) i -> p t i", t=PACK)
-        y01 = keep.tile([P, 2, I], F32, name="y01")
-        y23 = keep.tile([P, 2, I], F32, name="y23")
-        chunks = range(I // CHUNK)
-        y_bf = [keep.tile([P, CHUNK, PACK], BF16, name="y_bf%d" % k, align_bytes=64) for k in chunks]
+        y = keep.tile([P, PACK, I], F32, name="y")
+        pieces = [(0, 128), (128, 256), (256, 384), (384, 448)]
+        y_bf = [
+            keep.tile([P, hi - lo, PACK], BF16, name="y_bf%d" % k, tag="y_bf%d" % k, align_bytes=64)
+            for k, (lo, hi) in enumerate(pieces)
+        ]
         y_codes = keep.tile([P, I], U32, name="y_codes", align_bytes=64)
         y_scales = keep.tile([P, I], U8, name="y_scales", align_bytes=64)
 
-        for t in range(2):
-            nc.vector.tensor_tensor(y01[:, t, :], key_planes[t][:].indirect(offsets[:]), decoded[t][:], SUB)
-        nc.sync.dma_start(out=y_rows[:, 0:2, :], in_=y01[:])
-        for k in chunks:
-            cols = slice(CHUNK * k, CHUNK * (k + 1))
-            nc.scalar.copy(out=y_bf[k][:, :, 0:2], in_=y01[:, :, cols].rearrange("p t i -> p i t"))
-        nc.vector.tensor_tensor(y23[:, 0, :], key_planes[2][:].indirect(offsets[:]), decoded[2][:], SUB)
-        nc.scalar.dma_start(out=y_rows[:, 2, :], in_=y23[:, 0, :])
+        def round_pair(first, k):
+            lo, hi = pieces[k]
+            nc.scalar.copy(
+                out=y_bf[k][:, :, first : first + 2],
+                in_=y[:, first : first + 2, lo:hi].rearrange("p t i -> p i t"),
+            )
 
-        for k in chunks:
+        def quantise(source, lo, hi):
+            nc.vector.quantize_mx(
+                out=y_codes[:, lo:hi].bitcast(FP8X4),
+                scales=y_scales[:, lo:hi],
+                in_=source[:].rearrange("p i t -> p (i t)"),
+            )
+
+        for t in range(2):
+            nc.vector.tensor_tensor(y[:, t, :], key_planes[t][:].indirect(offsets[:]), decoded[t][:], SUB)
+        nc.sync.dma_start(out=y_rows[:, 0:2, :], in_=y[:, 0:2, :])
+        for k in range(4):
+            round_pair(0, k)
+        nc.vector.tensor_tensor(y[:, 2, :], key_planes[2][:].indirect(offsets[:]), decoded[2][:], SUB)
+        nc.scalar.dma_start(out=y_rows[:, 2, :], in_=y[:, 2, :])
+
+        for k in range(4):
             cols = slice(CHUNK * k, CHUNK * (k + 1))
             listed = offsets[:, CHUNK // 16 * k : CHUNK // 16 * (k + 1)]
-            nc.vector.tensor_tensor(y23[:, 1, cols], key_planes[3][:].indirect(listed), decoded[3][:, cols], SUB)
-            nc.scalar.copy(out=y_bf[k][:, :, 2:4], in_=y23[:, :, cols].rearrange("p t i -> p i t"))
-        nc.sync.dma_start(out=y_rows[:, 3, :], in_=y23[:, 1, :])
+            nc.vector.tensor_tensor(y[:, 3, cols], key_planes[3][:].indirect(listed), decoded[3][:, cols], SUB)
+            round_pair(2, k)
+        nc.sync.dma_start(out=y_rows[:, 3, :], in_=y[:, 3, :])
 
         word_rows = out_1[0].rearrange("p n t -> p (n t)").bitcast(I32)
-        for k in chunks:
-            cols = slice(CHUNK * k, CHUNK * (k + 1))
-            nc.vector.quantize_mx(
-                out=y_codes[:, cols].bitcast(FP8X4),
-                scales=y_scales[:, cols],
-                in_=y_bf[k][:].rearrange("p i t -> p (i t)"),
-            )
-            if k % 2 == 1:
-                half = slice(CHUNK * (k - 1), CHUNK * (k + 1))
-                queue = nc.scalar if k == 1 else nc.sync
-                queue.dma_start(out=word_rows[:, half], in_=y_codes[:, half].bitcast(I32))
+        quantise(y_bf[0], 0, 128)
+        quantise(y_bf[1], 128, 256)
+        nc.scalar.dma_start(out=word_rows[:, :256], in_=y_codes[:, :256].bitcast(I32))
+        y_end = keep.tile([P, 64, PACK], BF16, name="y_end", tag="y_bf0", align_bytes=64)
+        nc.vector.tensor_copy(out=y_end[:], in_=y[:, :, 448:].rearrange("p t i -> p i t"))
+        quantise(y_bf[2], 256, 384)
+        quantise(y_bf[3], 384, 448)
+        quantise(y_end, 448, 512)
+        nc.sync.dma_start(out=word_rows[:, 256:], in_=y_codes[:, 256:].bitcast(I32))
         for q in range(4):
             queue = nc.scalar if q % 2 == 0 else nc.sync
             queue.dma_start(

@@ -125,7 +125,9 @@ def tile_attend_residualcache_pl_kernel(tc, code_words, code_scales, dec, keys, 
             listed = offsets[:, CHUNK // 16 * k : CHUNK // 16 * (k + 1)]
             nc.vector.tensor_tensor(y[:, 3, cols], key_planes[3][:].indirect(listed), decoded[3][:, cols], SUB)
             round_pair(2, k)
-        nc.sync.dma_start(out=y_rows[:, 3, :], in_=y[:, 3, :])
+            if k % 2 == 1:
+                half = slice(CHUNK * (k - 1), CHUNK * (k + 1))
+                nc.sync.dma_start(out=y_rows[:, 3, half], in_=y[:, 3, half])
 
         word_rows = out_1[0].rearrange("p n t -> p (n t)").bitcast(I32)
         quantise(y_bf[0], 0, 128)
@@ -134,9 +136,10 @@ def tile_attend_residualcache_pl_kernel(tc, code_words, code_scales, dec, keys, 
         y_end = keep.tile([P, 64, PACK], BF16, name="y_end", tag="y_bf0", align_bytes=64)
         nc.vector.tensor_copy(out=y_end[:], in_=y[:, :, 448:].rearrange("p t i -> p i t"))
         quantise(y_bf[2], 256, 384)
+        nc.sync.dma_start(out=word_rows[:, 256:384], in_=y_codes[:, 256:384].bitcast(I32))
         quantise(y_bf[3], 384, 448)
         quantise(y_end, 448, 512)
-        nc.sync.dma_start(out=word_rows[:, 256:], in_=y_codes[:, 256:].bitcast(I32))
+        nc.sync.dma_start(out=word_rows[:, 384:], in_=y_codes[:, 384:].bitcast(I32))
         for q in range(4):
             queue = nc.scalar if q % 2 == 0 else nc.sync
             queue.dma_start(

@@ -114,7 +114,7 @@ def tile_attend_residualcache_pl_kernel(tc, code_words, code_scales, dec, keys, 
 
         for t in range(2):
             nc.vector.tensor_tensor(y[:, t, :], key_planes[t][:].indirect(offsets[:]), decoded[t][:], SUB)
-        nc.sync.dma_start(out=y_rows[:, 0:2, :], in_=y[:, 0:2, :])
+            nc.sync.dma_start(out=y_rows[:, t, :], in_=y[:, t, :])
         for k in range(4):
             round_pair(0, k)
         nc.vector.tensor_tensor(y[:, 2, :], key_planes[2][:].indirect(offsets[:]), decoded[2][:], SUB)
@@ -136,10 +136,9 @@ def tile_attend_residualcache_pl_kernel(tc, code_words, code_scales, dec, keys, 
         y_end = keep.tile([P, 64, PACK], BF16, name="y_end", tag="y_bf0", align_bytes=64)
         nc.vector.tensor_copy(out=y_end[:], in_=y[:, :, 448:].rearrange("p t i -> p i t"))
         quantise(y_bf[2], 256, 384)
-        nc.sync.dma_start(out=word_rows[:, 256:384], in_=y_codes[:, 256:384].bitcast(I32))
         quantise(y_bf[3], 384, 448)
         quantise(y_end, 448, 512)
-        nc.sync.dma_start(out=word_rows[:, 384:], in_=y_codes[:, 384:].bitcast(I32))
+        nc.sync.dma_start(out=word_rows[:, 256:], in_=y_codes[:, 256:].bitcast(I32))
         for q in range(4):
             queue = nc.scalar if q % 2 == 0 else nc.sync
             queue.dma_start(

@@ -26,10 +26,10 @@ def tile_attend_residualcache_pl_kernel(tc, code_words, code_scales, dec, keys, 
         keep = ctx.enter_context(tc.tile_pool(name="keep", bufs=1))
         psum = ctx.enter_context(tc.psum_pool(name="psum", bufs=1))
 
-        offsets = keep.tile([P, I // 16], U16, name="offsets")
-        dec_raw = keep.tile([P, PACK * D], F32, name="dec_raw", tag="slot_a")
-        words = keep.tile([P, T], U32, name="words", tag="slot_b")
-        scales = keep.tile([P, T], U8, name="scales", tag="slot_c")
+        offsets = keep.tile([P, I // 16], U16, name="offsets", align_bytes=256)
+        dec_raw = keep.tile([P, PACK * D], F32, name="dec_raw", tag="slot_a", align_bytes=256)
+        words = keep.tile([P, T], U32, name="words", tag="slot_b", align_bytes=256)
+        scales = keep.tile([P, T], U8, name="scales", tag="slot_c", align_bytes=256)
 
         nc.vector.memset(scales[:].bitcast(I32), 0)
         nc.sync.dma_start(out=dec_raw[:], in_=dec.rearrange("(p j) d -> p (j d)", j=PACK))
@@ -42,32 +42,32 @@ def tile_attend_residualcache_pl_kernel(tc, code_words, code_scales, dec, keys, 
         key_rows = keys.rearrange("(p t) n -> t p n", t=PACK)
         key_planes = []
         for t in range(1):
-            plane = keep.tile([P, T], F32, name="keys%d" % t)
+            plane = keep.tile([P, T], F32, name="keys%d" % t, align_bytes=256)
             nc.sync.dma_start(out=plane[:], in_=key_rows[t])
             key_planes.append(plane)
 
-        dec_bf = keep.tile([P, D * PACK], BF16, name="dec_bf", align_bytes=64)
+        dec_bf = keep.tile([P, D * PACK], BF16, name="dec_bf", align_bytes=256)
         dealt = dec_bf[:].rearrange("p (t m j) -> p m t j", t=PACK, j=PACK)
         source = dec_raw[:].rearrange("p (j m t) -> p m t j", j=PACK, t=PACK)
         nc.scalar.copy(out=dealt[:, :SCALAR_M], in_=source[:, :SCALAR_M])
         nc.vector.tensor_copy(out=dealt[:, SCALAR_M:], in_=source[:, SCALAR_M:])
-        scales_s = keep.tile([P, I], U8, name="scales_s", align_bytes=64)
+        scales_s = keep.tile([P, I], U8, name="scales_s", align_bytes=256)
         nc.vector.tensor_copy(scales_s[:], scales[:].indirect(offsets[:]))
-        scales_g = keep.tile([P, I], U8, name="scales_g", align_bytes=64)
+        scales_g = keep.tile([P, I], U8, name="scales_g", align_bytes=256)
         nc.vector.memset(scales_g[:].bitcast(I32), 0)
         for r in range(4):
             nc.sync.dma_start(
                 out=scales_g[r:P:32, :].bitcast(I32),
                 in_=scales_s[32 + 4 * r : 96 : 16, :].bitcast(I32),
             )
-        words_g = keep.tile([P, I], U32, name="words_g", align_bytes=64)
+        words_g = keep.tile([P, I], U32, name="words_g", align_bytes=256)
         nc.vector.tensor_copy(words_g[:], words[:].indirect(offsets[:]))
-        dec_codes = keep.tile([P, D], U32, name="dec_codes", align_bytes=64)
-        dec_scales = keep.tile([P, D], U8, name="dec_scales", align_bytes=64)
+        dec_codes = keep.tile([P, D], U32, name="dec_codes", align_bytes=256)
+        dec_scales = keep.tile([P, D], U8, name="dec_scales", align_bytes=256)
         nc.vector.quantize_mx(out=dec_codes[:].bitcast(FP8X4), scales=dec_scales[:], in_=dec_bf[:])
 
         for t, tag in ((1, "slot_c"), (2, "slot_a"), (3, "slot_b")):
-            plane = keep.tile([P, T], F32, name="keys%d" % t, tag=tag)
+            plane = keep.tile([P, T], F32, name="keys%d" % t, tag=tag, align_bytes=256)
             nc.sync.dma_start(out=plane[:], in_=key_rows[t])
             key_planes.append(plane)
 
@@ -84,19 +84,19 @@ def tile_attend_residualcache_pl_kernel(tc, code_words, code_scales, dec, keys, 
                 start=True,
                 stop=True,
             )
-            b = keep.tile([P, I], F32, name="b%d" % t)
+            b = keep.tile([P, I], F32, name="b%d" % t, align_bytes=256)
             nc.scalar.copy(out=b[:], in_=acc[:])
             decoded.append(b)
 
         y_rows = out_0.rearrange("(p t) i -> p t i", t=PACK)
-        y = keep.tile([P, PACK, I], F32, name="y")
+        y = keep.tile([P, PACK, I], F32, name="y", align_bytes=256)
         pieces = [(0, 128), (128, 256), (256, 384), (384, 448)]
         y_bf = [
-            keep.tile([P, hi - lo, PACK], BF16, name="y_bf%d" % k, tag="y_bf%d" % k, align_bytes=64)
+            keep.tile([P, hi - lo, PACK], BF16, name="y_bf%d" % k, tag="y_bf%d" % k, align_bytes=256)
             for k, (lo, hi) in enumerate(pieces)
         ]
-        y_codes = keep.tile([P, I], U32, name="y_codes", align_bytes=64)
-        y_scales = keep.tile([P, I], U8, name="y_scales", align_bytes=64)
+        y_codes = keep.tile([P, I], U32, name="y_codes", align_bytes=256)
+        y_scales = keep.tile([P, I], U8, name="y_scales", align_bytes=256)
 
         def round_pair(first, k):
             lo, hi = pieces[k]
@@ -133,7 +133,7 @@ def tile_attend_residualcache_pl_kernel(tc, code_words, code_scales, dec, keys, 
         quantise(y_bf[0], 0, 128)
         quantise(y_bf[1], 128, 256)
         nc.scalar.dma_start(out=word_rows[:, :256], in_=y_codes[:, :256].bitcast(I32))
-        y_end = keep.tile([P, 64, PACK], BF16, name="y_end", tag="y_bf0", align_bytes=64)
+        y_end = keep.tile([P, 64, PACK], BF16, name="y_end", tag="y_bf0", align_bytes=256)
         nc.vector.tensor_copy(out=y_end[:], in_=y[:, :, 448:].rearrange("p t i -> p i t"))
         quantise(y_bf[2], 256, 384)
         quantise(y_bf[3], 384, 448)

@@ -114,7 +114,7 @@ def tile_attend_residualcache_pl_kernel(tc, code_words, code_scales, dec, keys, 
 
         for t in range(2):
             nc.vector.tensor_tensor(y[:, t, :], key_planes[t][:].indirect(offsets[:]), decoded[t][:], SUB)
-            nc.sync.dma_start(out=y_rows[:, t, :], in_=y[:, t, :])
+        nc.sync.dma_start(out=y_rows[:, :2, :], in_=y[:, :2, :])
         for k in range(4):
             round_pair(0, k)
         nc.vector.tensor_tensor(y[:, 2, :], key_planes[2][:].indirect(offsets[:]), decoded[2][:], SUB)
@@ -125,9 +125,9 @@ def tile_attend_residualcache_pl_kernel(tc, code_words, code_scales, dec, keys, 
             listed = offsets[:, CHUNK // 16 * k : CHUNK // 16 * (k + 1)]
             nc.vector.tensor_tensor(y[:, 3, cols], key_planes[3][:].indirect(listed), decoded[3][:, cols], SUB)
             round_pair(2, k)
-            if k % 2 == 1:
-                half = slice(CHUNK * (k - 1), CHUNK * (k + 1))
-                nc.sync.dma_start(out=y_rows[:, 3, half], in_=y[:, 3, half])
+            if k == 0:
+                nc.sync.dma_start(out=y_rows[:, 3, :CHUNK], in_=y[:, 3, :CHUNK])
+        nc.sync.dma_start(out=y_rows[:, 3, CHUNK:], in_=y[:, 3, CHUNK:])
 
         word_rows = out_1[0].rearrange("p n t -> p (n t)").bitcast(I32)
         quantise(y_bf[0], 0, 128)
@@ -136,9 +136,10 @@ def tile_attend_residualcache_pl_kernel(tc, code_words, code_scales, dec, keys, 
         y_end = keep.tile([P, 64, PACK], BF16, name="y_end", tag="y_bf0", align_bytes=256)
         nc.vector.tensor_copy(out=y_end[:], in_=y[:, :, 448:].rearrange("p t i -> p i t"))
         quantise(y_bf[2], 256, 384)
+        nc.sync.dma_start(out=word_rows[:, 256:384], in_=y_codes[:, 256:384].bitcast(I32))
         quantise(y_bf[3], 384, 448)
         quantise(y_end, 448, 512)
-        nc.sync.dma_start(out=word_rows[:, 256:], in_=y_codes[:, 256:].bitcast(I32))
+        nc.sync.dma_start(out=word_rows[:, 384:], in_=y_codes[:, 384:].bitcast(I32))
         for q in range(4):
             queue = nc.scalar if q % 2 == 0 else nc.sync
             queue.dma_start(

@@ -26,10 +26,10 @@ def tile_attend_residualcache_pl_kernel(tc, code_words, code_scales, dec, keys, 
         keep = ctx.enter_context(tc.tile_pool(name="keep", bufs=1))
         psum = ctx.enter_context(tc.psum_pool(name="psum", bufs=1))
 
-        offsets = keep.tile([P, I // 16], U16, name="offsets", align_bytes=256)
-        dec_raw = keep.tile([P, PACK * D], F32, name="dec_raw", tag="slot_a", align_bytes=256)
-        words = keep.tile([P, T], U32, name="words", tag="slot_b", align_bytes=256)
-        scales = keep.tile([P, T], U8, name="scales", tag="slot_c", align_bytes=256)
+        offsets = keep.tile([P, I // 16], U16, name="offsets", align_bytes=4096)
+        dec_raw = keep.tile([P, PACK * D], F32, name="dec_raw", tag="slot_a", align_bytes=4096)
+        words = keep.tile([P, T], U32, name="words", tag="slot_b", align_bytes=4096)
+        scales = keep.tile([P, T], U8, name="scales", tag="slot_c", align_bytes=4096)
 
         nc.vector.memset(scales[:].bitcast(I32), 0)
         nc.sync.dma_start(out=dec_raw[:], in_=dec.rearrange("(p j) d -> p (j d)", j=PACK))
@@ -42,32 +42,32 @@ def tile_attend_residualcache_pl_kernel(tc, code_words, code_scales, dec, keys, 
         key_rows = keys.rearrange("(p t) n -> t p n", t=PACK)
         key_planes = []
         for t in range(1):
-            plane = keep.tile([P, T], F32, name="keys%d" % t, align_bytes=256)
+            plane = keep.tile([P, T], F32, name="keys%d" % t, align_bytes=4096)
             nc.sync.dma_start(out=plane[:], in_=key_rows[t])
             key_planes.append(plane)
 
-        dec_bf = keep.tile([P, D * PACK], BF16, name="dec_bf", align_bytes=256)
+        dec_bf = keep.tile([P, D * PACK], BF16, name="dec_bf", align_bytes=4096)
         dealt = dec_bf[:].rearrange("p (t m j) -> p m t j", t=PACK, j=PACK)
         source = dec_raw[:].rearrange("p (j m t) -> p m t j", j=PACK, t=PACK)
         nc.scalar.copy(out=dealt[:, :SCALAR_M], in_=source[:, :SCALAR_M])
         nc.vector.tensor_copy(out=dealt[:, SCALAR_M:], in_=source[:, SCALAR_M:])
-        scales_s = keep.tile([P, I], U8, name="scales_s", align_bytes=256)
+        scales_s = keep.tile([P, I], U8, name="scales_s", align_bytes=4096)
         nc.vector.tensor_copy(scales_s[:], scales[:].indirect(offsets[:]))
-        scales_g = keep.tile([P, I], U8, name="scales_g", align_bytes=256)
+        scales_g = keep.tile([P, I], U8, name="scales_g", align_bytes=4096)
         nc.vector.memset(scales_g[:].bitcast(I32), 0)
         for r in range(4):
             nc.sync.dma_start(
                 out=scales_g[r:P:32, :].bitcast(I32),
                 in_=scales_s[32 + 4 * r : 96 : 16, :].bitcast(I32),
             )
-        words_g = keep.tile([P, I], U32, name="words_g", align_bytes=256)
+        words_g = keep.tile([P, I], U32, name="words_g", align_bytes=4096)
         nc.vector.tensor_copy(words_g[:], words[:].indirect(offsets[:]))
-        dec_codes = keep.tile([P, D], U32, name="dec_codes", align_bytes=256)
-        dec_scales = keep.tile([P, D], U8, name="dec_scales", align_bytes=256)
+        dec_codes = keep.tile([P, D], U32, name="dec_codes", align_bytes=4096)
+        dec_scales = keep.tile([P, D], U8, name="dec_scales", align_bytes=4096)
         nc.vector.quantize_mx(out=dec_codes[:].bitcast(FP8X4), scales=dec_scales[:], in_=dec_bf[:])
 
         for t, tag in ((1, "slot_c"), (2, "slot_a"), (3, "slot_b")):
-            plane = keep.tile([P, T], F32, name="keys%d" % t, tag=tag, align_bytes=256)
+            plane = keep.tile([P, T], F32, name="keys%d" % t, tag=tag, align_bytes=4096)
             nc.sync.dma_start(out=plane[:], in_=key_rows[t])
             key_planes.append(plane)
 
@@ -84,19 +84,19 @@ def tile_attend_residualcache_pl_kernel(tc, code_words, code_scales, dec, keys, 
                 start=True,
                 stop=True,
             )
-            b = keep.tile([P, I], F32, name="b%d" % t, align_bytes=256)
+            b = keep.tile([P, I], F32, name="b%d" % t, align_bytes=4096)
             nc.scalar.copy(out=b[:], in_=acc[:])
             decoded.append(b)
 
         y_rows = out_0.rearrange("(p t) i -> p t i", t=PACK)
-        y = keep.tile([P, PACK, I], F32, name="y", align_bytes=256)
+        y = keep.tile([P, PACK, I], F32, name="y", align_bytes=4096)
         pieces = [(0, 128), (128, 256), (256, 384), (384, 448)]
         y_bf = [
-            keep.tile([P, hi - lo, PACK], BF16, name="y_bf%d" % k, tag="y_bf%d" % k, align_bytes=256)
+            keep.tile([P, hi - lo, PACK], BF16, name="y_bf%d" % k, tag="y_bf%d" % k, align_bytes=4096)
             for k, (lo, hi) in enumerate(pieces)
         ]
-        y_codes = keep.tile([P, I], U32, name="y_codes", align_bytes=256)
-        y_scales = keep.tile([P, I], U8, name="y_scales", align_bytes=256)
+        y_codes = keep.tile([P, I], U32, name="y_codes", align_bytes=4096)
+        y_scales = keep.tile([P, I], U8, name="y_scales", align_bytes=4096)
 
         def round_pair(first, k):
             lo, hi = pieces[k]
@@ -133,7 +133,7 @@ def tile_attend_residualcache_pl_kernel(tc, code_words, code_scales, dec, keys, 
         quantise(y_bf[0], 0, 128)
         quantise(y_bf[1], 128, 256)
         nc.scalar.dma_start(out=word_rows[:, :256], in_=y_codes[:, :256].bitcast(I32))
-        y_end = keep.tile([P, 64, PACK], BF16, name="y_end", tag="y_bf0", align_bytes=256)
+        y_end = keep.tile([P, 64, PACK], BF16, name="y_end", tag="y_bf0", align_bytes=4096)
         nc.vector.tensor_copy(out=y_end[:], in_=y[:, :, 448:].rearrange("p t i -> p i t"))
         quantise(y_bf[2], 256, 384)
         nc.sync.dma_start(out=word_rows[:, 256:384], in_=y_codes[:, 256:384].bitcast(I32))

@@ -13,6 +13,7 @@ U16 = mybir.dt.uint16
 U8 = mybir.dt.uint8
 FP8X4 = mybir.dt.float8_e4m3fn_x4
 SUB = mybir.AluOpType.subtract
+COPY = mybir.ActivationFunctionType.Copy
 
 P = 128
 PACK = 4
@@ -40,11 +41,9 @@ def tile_attend_residualcache_pl_kernel(tc, code_words, code_scales, dec, keys, 
             in_=code_words[0].rearrange("p n t -> p (n t)").bitcast(I32),
         )
         key_rows = keys.rearrange("(p t) n -> t p n", t=PACK)
-        key_planes = []
-        for t in range(1):
-            plane = keep.tile([P, T], F32, name="keys%d" % t, align_bytes=4096)
-            nc.sync.dma_start(out=plane[:], in_=key_rows[t])
-            key_planes.append(plane)
+        keys01 = keep.tile([P, 2 * T], F32, name="keys01", align_bytes=4096)
+        nc.sync.dma_start(out=keys01[:], in_=keys.rearrange("(p u t) n -> u p (t n)", u=2, t=2)[0])
+        key_planes = {}
 
         dec_bf = keep.tile([P, D * PACK], BF16, name="dec_bf", align_bytes=4096)
         dealt = dec_bf[:].rearrange("p (t m j) -> p m t j", t=PACK, j=PACK)
@@ -66,10 +65,14 @@ def tile_attend_residualcache_pl_kernel(tc, code_words, code_scales, dec, keys, 
         dec_scales = keep.tile([P, D], U8, name="dec_scales", align_bytes=4096)
         nc.vector.quantize_mx(out=dec_codes[:].bitcast(FP8X4), scales=dec_scales[:], in_=dec_bf[:])
 
-        for t, tag in ((1, "slot_c"), (2, "slot_a"), (3, "slot_b")):
+        for t, tag in ((2, "slot_c"), (3, "slot_b")):
             plane = keep.tile([P, T], F32, name="keys%d" % t, tag=tag, align_bytes=4096)
             nc.sync.dma_start(out=plane[:], in_=key_rows[t])
-            key_planes.append(plane)
+            key_planes[t] = plane
+
+        picked = [keep.tile([P, I], F32, name="picked%d" % t, align_bytes=4096) for t in range(2)]
+        nc.vector.tensor_copy(picked[0][:], keys01[:, :T].indirect(offsets[:]))
+        nc.scalar.activation(picked[1][:], keys01[:, T:].indirect(offsets[:]), COPY)
 
         decoded = []
         for t in range(PACK):
@@ -84,9 +87,12 @@ def tile_attend_residualcache_pl_kernel(tc, code_words, code_scales, dec, keys, 
                 start=True,
                 stop=True,
             )
-            b = keep.tile([P, I], F32, name="b%d" % t, align_bytes=4096)
-            nc.scalar.copy(out=b[:], in_=acc[:])
-            decoded.append(b)
+            if t < 2:
+                decoded.append(acc)
+            else:
+                b = keep.tile([P, I], F32, name="b%d" % t, align_bytes=4096)
+                nc.scalar.copy(out=b[:], in_=acc[:])
+                decoded.append(b)
 
         y_rows = out_0.rearrange("(p t) i -> p t i", t=PACK)
         y = keep.tile([P, PACK, I], F32, name="y", align_bytes=4096)
@@ -113,8 +119,8 @@ def tile_attend_residualcache_pl_kernel(tc, code_words, code_scales, dec, keys, 
             )
 
         for t in range(2):
-            nc.vector.tensor_tensor(y[:, t, :], key_planes[t][:].indirect(offsets[:]), decoded[t][:], SUB)
-        nc.sync.dma_start(out=y_rows[:, :2, :], in_=y[:, :2, :])
+            nc.vector.tensor_tensor(y[:, t, :], picked[t][:], decoded[t][:], SUB)
+            nc.sync.dma_start(out=y_rows[:, t, :], in_=y[:, t, :])
         for k in range(4):
             round_pair(0, k)
         nc.vector.tensor_tensor(y[:, 2, :], key_planes[2][:].indirect(offsets[:]), decoded[2][:], SUB)
@@ -143,6 +149,6 @@ def tile_attend_residualcache_pl_kernel(tc, code_words, code_scales, dec, keys, 
         for q in range(4):
             queue = nc.scalar if q % 2 == 0 else nc.sync
             queue.dma_start(
-                out=out_2[0, 4 * q : 4 * q + 4, :].bitcast(I32),
-                in_=y_scales[32 * q : 32 * q + 4, :].bitcast(I32),
+                out=out_2[0, q:16:4, :].bitcast(I32),
+                in_=y_scales[q:P:32, :].bitcast(I32),
             )

@@ -19,6 +19,8 @@ P = 128
 PACK = 4
 CHUNK = 128
 SCALAR_M = 80
+SPLIT = 320
+PLANE2_CUTS = ((0, 384), (384, 512))
 
 
 def tile_attend_residualcache_pl_kernel(tc, code_words, code_scales, dec, keys, offs, out_0, out_1, out_2):
@@ -75,6 +77,7 @@ def tile_attend_residualcache_pl_kernel(tc, code_words, code_scales, dec, keys, 
         nc.scalar.activation(picked[1][:], keys01[:, T:].indirect(offsets[:]), COPY)
 
         decoded = []
+        sums = []
         for t in range(PACK):
             cols = slice(P * t, P * (t + 1))
             acc = psum.tile([P, I], F32, name="acc%d" % t)
@@ -87,68 +90,85 @@ def tile_attend_residualcache_pl_kernel(tc, code_words, code_scales, dec, keys, 
                 start=True,
                 stop=True,
             )
-            if t < 2:
+            sums.append(acc)
+            if t == 2:
+                halves = []
+                for lo, hi in PLANE2_CUTS:
+                    half = keep.tile([P, hi - lo], F32, name="picked2_%d" % lo, align_bytes=4096)
+                    cols = offsets[:, lo // 16 : hi // 16]
+                    nc.scalar.activation(half[:], key_planes[2][:].indirect(cols), COPY)
+                    halves.append(half)
+            if t < 3:
                 decoded.append(acc)
             else:
-                b = keep.tile([P, I], F32, name="b%d" % t, align_bytes=4096)
-                nc.scalar.copy(out=b[:], in_=acc[:])
+                b = keep.tile([P, SPLIT], F32, name="b%d" % t, tag="slot_c", align_bytes=4096)
+                nc.scalar.copy(out=b[:, :CHUNK], in_=acc[:, :CHUNK])
+                nc.scalar.copy(out=b[:, CHUNK:], in_=acc[:, CHUNK:SPLIT])
                 decoded.append(b)
 
         y_rows = out_0.rearrange("(p t) i -> p t i", t=PACK)
         y = keep.tile([P, PACK, I], F32, name="y", align_bytes=4096)
-        pieces = [(0, 128), (128, 256), (256, 384), (384, 448)]
+        pieces = [(0, 128), (128, 256), (256, 320), (320, 448), (448, 512)]
         y_bf = [
-            keep.tile([P, hi - lo, PACK], BF16, name="y_bf%d" % k, tag="y_bf%d" % k, align_bytes=4096)
+            keep.tile([P, hi - lo, PACK], BF16, name="y_bf%d" % k, align_bytes=4096)
             for k, (lo, hi) in enumerate(pieces)
         ]
         y_codes = keep.tile([P, I], U32, name="y_codes", align_bytes=4096)
         y_scales = keep.tile([P, I], U8, name="y_scales", align_bytes=4096)
+        word_rows = out_1[0].rearrange("p n t -> p (n t)").bitcast(I32)
 
-        def round_pair(first, k):
+        def listed(lo, hi):
+            return offsets[:, lo // 16 : hi // 16]
+
+        def round_pair(copy, first, k):
             lo, hi = pieces[k]
-            nc.scalar.copy(
+            copy(
                 out=y_bf[k][:, :, first : first + 2],
                 in_=y[:, first : first + 2, lo:hi].rearrange("p t i -> p i t"),
             )
 
-        def quantise(source, lo, hi):
+        def quantise(k):
+            lo, hi = pieces[k]
             nc.vector.quantize_mx(
                 out=y_codes[:, lo:hi].bitcast(FP8X4),
                 scales=y_scales[:, lo:hi],
-                in_=source[:].rearrange("p i t -> p (i t)"),
+                in_=y_bf[k][:].rearrange("p i t -> p (i t)"),
             )
 
         for t in range(2):
             nc.vector.tensor_tensor(y[:, t, :], picked[t][:], decoded[t][:], SUB)
             nc.sync.dma_start(out=y_rows[:, t, :], in_=y[:, t, :])
-        for k in range(4):
-            round_pair(0, k)
-        nc.vector.tensor_tensor(y[:, 2, :], key_planes[2][:].indirect(offsets[:]), decoded[2][:], SUB)
-        nc.scalar.dma_start(out=y_rows[:, 2, :], in_=y[:, 2, :])
+        for k in range(len(pieces)):
+            round_pair(nc.vector.tensor_copy, 0, k)
+        for half, (lo, hi) in zip(halves, PLANE2_CUTS):
+            nc.vector.tensor_tensor(y[:, 2, lo:hi], half[:], decoded[2][:, lo:hi], SUB)
+        nc.sync.dma_start(out=y_rows[:, 2, :], in_=y[:, 2, :])
 
-        for k in range(4):
-            cols = slice(CHUNK * k, CHUNK * (k + 1))
-            listed = offsets[:, CHUNK // 16 * k : CHUNK // 16 * (k + 1)]
-            nc.vector.tensor_tensor(y[:, 3, cols], key_planes[3][:].indirect(listed), decoded[3][:, cols], SUB)
-            round_pair(2, k)
-            if k == 0:
+        last = key_planes[3]
+        picked3 = keep.tile([P, I - SPLIT], F32, name="picked3", align_bytes=4096)
+        nc.scalar.activation(picked3[:], last[:].indirect(listed(SPLIT, I)), COPY)
+        for lo, hi in ((0, CHUNK), (CHUNK, SPLIT)):
+            nc.vector.tensor_tensor(y[:, 3, lo:hi], last[:].indirect(listed(lo, hi)), decoded[3][:, lo:hi], SUB)
+            if lo == 0:
                 nc.sync.dma_start(out=y_rows[:, 3, :CHUNK], in_=y[:, 3, :CHUNK])
+        nc.vector.tensor_tensor(y[:, 3, SPLIT:], picked3[:], sums[3][:, SPLIT:], SUB)
         nc.sync.dma_start(out=y_rows[:, 3, CHUNK:], in_=y[:, 3, CHUNK:])
-
-        word_rows = out_1[0].rearrange("p n t -> p (n t)").bitcast(I32)
-        quantise(y_bf[0], 0, 128)
-        quantise(y_bf[1], 128, 256)
-        nc.scalar.dma_start(out=word_rows[:, :256], in_=y_codes[:, :256].bitcast(I32))
-        y_end = keep.tile([P, 64, PACK], BF16, name="y_end", tag="y_bf0", align_bytes=4096)
-        nc.vector.tensor_copy(out=y_end[:], in_=y[:, :, 448:].rearrange("p t i -> p i t"))
-        quantise(y_bf[2], 256, 384)
-        nc.sync.dma_start(out=word_rows[:, 256:384], in_=y_codes[:, 256:384].bitcast(I32))
-        quantise(y_bf[3], 384, 448)
-        quantise(y_end, 448, 512)
-        nc.sync.dma_start(out=word_rows[:, 384:], in_=y_codes[:, 384:].bitcast(I32))
-        for q in range(4):
-            queue = nc.scalar if q % 2 == 0 else nc.sync
+        round_pair(nc.scalar.copy, 2, 0)
+        round_pair(nc.scalar.copy, 2, 1)
+        round_pair(nc.vector.tensor_copy, 2, 2)
+        quantise(0)
+        nc.sync.dma_start(out=word_rows[:, :128], in_=y_codes[:, :128].bitcast(I32))
+        round_pair(nc.vector.tensor_copy, 2, 3)
+        round_pair(nc.scalar.copy, 2, 4)
+        quantise(2)
+        quantise(1)
+        nc.sync.dma_start(out=word_rows[:, 128:320], in_=y_codes[:, 128:320].bitcast(I32))
+        quantise(3)
+        quantise(4)
+        nc.sync.dma_start(out=word_rows[:, 320:], in_=y_codes[:, 320:].bitcast(I32))
+        for r in range(4):
+            queue = nc.scalar if r % 2 == 0 else nc.sync
             queue.dma_start(
-                out=out_2[0, q:16:4, :].bitcast(I32),
-                in_=y_scales[q:P:32, :].bitcast(I32),
+                out=out_2[0, r:16:4, :].bitcast(I32),
+                in_=y_scales[r:P:32, :].bitcast(I32),
             )

@@ -76,21 +76,26 @@ def tile_attend_residualcache_pl_kernel(tc, code_words, code_scales, dec, keys, 
         nc.vector.tensor_copy(picked[0][:], keys01[:, :T].indirect(offsets[:]))
         nc.scalar.activation(picked[1][:], keys01[:, T:].indirect(offsets[:]), COPY)
 
-        decoded = []
-        sums = []
-        for t in range(PACK):
+        def product(t, lo, hi):
             cols = slice(P * t, P * (t + 1))
-            acc = psum.tile([P, I], F32, name="acc%d" % t)
+            acc = psum.tile([P, hi - lo], F32, name="acc%d_%d" % (t, lo))
             nc.tensor.matmul_mx(
                 out=acc[:],
                 lhsT=dec_codes[:, cols].bitcast(FP8X4),
                 lhsT_scale=dec_scales[:, cols],
-                rhs=words_g[:].bitcast(FP8X4),
-                rhs_scale=scales_g[:],
+                rhs=words_g[:, lo:hi].bitcast(FP8X4),
+                rhs_scale=scales_g[:, lo:hi],
                 start=True,
                 stop=True,
             )
-            sums.append(acc)
+            return acc
+
+        early = {(t, lo): product(t, lo, lo + I // 2) for lo in (0, I // 2) for t in range(2)}
+        decoded = {}
+        sums = {}
+        for t in range(2, PACK):
+            acc = product(t, 0, I)
+            sums[t] = acc
             if t == 2:
                 halves = []
                 for lo, hi in PLANE2_CUTS:
@@ -99,12 +104,12 @@ def tile_attend_residualcache_pl_kernel(tc, code_words, code_scales, dec, keys, 
                     nc.scalar.activation(half[:], key_planes[2][:].indirect(cols), COPY)
                     halves.append(half)
             if t < 3:
-                decoded.append(acc)
+                decoded[t] = acc
             else:
                 b = keep.tile([P, SPLIT], F32, name="b%d" % t, tag="slot_c", align_bytes=4096)
                 nc.scalar.copy(out=b[:, :CHUNK], in_=acc[:, :CHUNK])
                 nc.scalar.copy(out=b[:, CHUNK:], in_=acc[:, CHUNK:SPLIT])
-                decoded.append(b)
+                decoded[t] = b
 
         y_rows = out_0.rearrange("(p t) i -> p t i", t=PACK)
         y = keep.tile([P, PACK, I], F32, name="y", align_bytes=4096)
@@ -135,8 +140,11 @@ def tile_attend_residualcache_pl_kernel(tc, code_words, code_scales, dec, keys, 
                 in_=y_bf[k][:].rearrange("p i t -> p (i t)"),
             )
 
+        for lo in (0, I // 2):
+            cols = slice(lo, lo + I // 2)
+            for t in range(2):
+                nc.vector.tensor_tensor(y[:, t, cols], picked[t][:, cols], early[t, lo][:], SUB)
         for t in range(2):
-            nc.vector.tensor_tensor(y[:, t, :], picked[t][:], decoded[t][:], SUB)
             nc.sync.dma_start(out=y_rows[:, t, :], in_=y[:, t, :])
         for k in range(len(pieces)):
             round_pair(nc.vector.tensor_copy, 0, k)

@@ -37,7 +37,7 @@ def tile_attend_residualcache_pl_kernel(tc, code_words, code_scales, dec, keys, 
         nc.vector.memset(scales[:].bitcast(I32), 0)
         nc.sync.dma_start(out=dec_raw[:], in_=dec.rearrange("(p j) d -> p (j d)", j=PACK))
         nc.sync.dma_start(offsets[:], offs)
-        nc.sync.dma_start(out=scales[32:96:4, :].bitcast(I32), in_=code_scales[0].bitcast(I32))
+        nc.sync.dma_start(out=scales[0:P:8, :].bitcast(I32), in_=code_scales[0].bitcast(I32))
         nc.sync.dma_start(
             out=words[:].bitcast(I32),
             in_=code_words[0].rearrange("p n t -> p (n t)").bitcast(I32),
@@ -55,11 +55,11 @@ def tile_attend_residualcache_pl_kernel(tc, code_words, code_scales, dec, keys, 
         scales_s = keep.tile([P, I], U8, name="scales_s", align_bytes=4096)
         nc.vector.tensor_copy(scales_s[:], scales[:].indirect(offsets[:]))
         scales_g = keep.tile([P, I], U8, name="scales_g", align_bytes=4096)
-        nc.vector.memset(scales_g[:].bitcast(I32), 0)
-        for r in range(4):
+        nc.vector.tensor_copy(out=scales_g[:].bitcast(I32), in_=scales_s[:].bitcast(I32))
+        for r in range(1, 4):
             nc.sync.dma_start(
                 out=scales_g[r:P:32, :].bitcast(I32),
-                in_=scales_s[32 + 4 * r : 96 : 16, :].bitcast(I32),
+                in_=scales_s[8 * r : P : 32, :].bitcast(I32),
             )
         words_g = keep.tile([P, I], U32, name="words_g", align_bytes=4096)
         nc.vector.tensor_copy(words_g[:], words[:].indirect(offsets[:]))

@@ -17,10 +17,12 @@ COPY = mybir.ActivationFunctionType.Copy
 
 P = 128
 PACK = 4
-CHUNK = 128
+ALIGN = 4096
+HALF = I // 2
 SCALAR_M = 80
+FIRST = 128
 SPLIT = 320
-PLANE2_CUTS = ((0, 384), (384, 512))
+PLANE2_CUT = 384
 
 
 def tile_attend_residualcache_pl_kernel(tc, code_words, code_scales, dec, keys, offs, out_0, out_1, out_2):
@@ -29,52 +31,52 @@ def tile_attend_residualcache_pl_kernel(tc, code_words, code_scales, dec, keys, 
         keep = ctx.enter_context(tc.tile_pool(name="keep", bufs=1))
         psum = ctx.enter_context(tc.psum_pool(name="psum", bufs=1))
 
-        offsets = keep.tile([P, I // 16], U16, name="offsets", align_bytes=4096)
-        dec_raw = keep.tile([P, PACK * D], F32, name="dec_raw", tag="slot_a", align_bytes=4096)
-        words = keep.tile([P, T], U32, name="words", tag="slot_b", align_bytes=4096)
-        scales = keep.tile([P, T], U8, name="scales", tag="slot_c", align_bytes=4096)
+        def tile(shape, dtype, name, tag=None):
+            return keep.tile(shape, dtype, name=name, tag=tag or name, align_bytes=ALIGN)
+
+        offsets = tile([P, I // 16], U16, "offsets")
+        words = tile([P, T], U32, "words")
+        scales = tile([P, T], U8, "scales")
+        dec_raw = tile([P, PACK * D], F32, "dec_raw")
+        keys01 = tile([P, 2 * T], F32, "keys01")
+
+        def listed(lo, hi):
+            return offsets[:, lo // 16 : hi // 16]
 
         nc.vector.memset(scales[:].bitcast(I32), 0)
-        nc.sync.dma_start(out=dec_raw[:], in_=dec.rearrange("(p j) d -> p (j d)", j=PACK))
+        nc.sync.dma_start(out=words[:].bitcast(I32), in_=code_words[0].rearrange("p n t -> p (n t)").bitcast(I32))
         nc.sync.dma_start(offsets[:], offs)
         nc.sync.dma_start(out=scales[0:P:8, :].bitcast(I32), in_=code_scales[0].bitcast(I32))
-        nc.sync.dma_start(
-            out=words[:].bitcast(I32),
-            in_=code_words[0].rearrange("p n t -> p (n t)").bitcast(I32),
-        )
-        key_rows = keys.rearrange("(p t) n -> t p n", t=PACK)
-        keys01 = keep.tile([P, 2 * T], F32, name="keys01", align_bytes=4096)
+        nc.sync.dma_start(out=dec_raw[:], in_=dec.rearrange("(p j) d -> p (j d)", j=PACK))
         nc.sync.dma_start(out=keys01[:], in_=keys.rearrange("(p u t) n -> u p (t n)", u=2, t=2)[0])
-        key_planes = {}
 
-        dec_bf = keep.tile([P, D * PACK], BF16, name="dec_bf", align_bytes=4096)
+        scales_s = tile([P, I], U8, "scales_s")
+        nc.vector.tensor_copy(scales_s[:], scales[:].indirect(offsets[:]))
+        scales_g = tile([P, I], U8, "scales_g")
+        nc.vector.tensor_copy(out=scales_g[:].bitcast(I32), in_=scales_s[:].bitcast(I32))
+        for r in range(1, 4):
+            nc.sync.dma_start(out=scales_g[r:P:32, :].bitcast(I32), in_=scales_s[8 * r : P : 32, :].bitcast(I32))
+        words_g = tile([P, I], U32, "words_g")
+        nc.vector.tensor_copy(words_g[:], words[:].indirect(offsets[:]))
+        dec_bf = tile([P, D * PACK], BF16, "dec_bf")
         dealt = dec_bf[:].rearrange("p (t m j) -> p m t j", t=PACK, j=PACK)
         source = dec_raw[:].rearrange("p (j m t) -> p m t j", j=PACK, t=PACK)
         nc.scalar.copy(out=dealt[:, :SCALAR_M], in_=source[:, :SCALAR_M])
         nc.vector.tensor_copy(out=dealt[:, SCALAR_M:], in_=source[:, SCALAR_M:])
-        scales_s = keep.tile([P, I], U8, name="scales_s", align_bytes=4096)
-        nc.vector.tensor_copy(scales_s[:], scales[:].indirect(offsets[:]))
-        scales_g = keep.tile([P, I], U8, name="scales_g", align_bytes=4096)
-        nc.vector.tensor_copy(out=scales_g[:].bitcast(I32), in_=scales_s[:].bitcast(I32))
-        for r in range(1, 4):
-            nc.sync.dma_start(
-                out=scales_g[r:P:32, :].bitcast(I32),
-                in_=scales_s[8 * r : P : 32, :].bitcast(I32),
-            )
-        words_g = keep.tile([P, I], U32, name="words_g", align_bytes=4096)
-        nc.vector.tensor_copy(words_g[:], words[:].indirect(offsets[:]))
-        dec_codes = keep.tile([P, D], U32, name="dec_codes", align_bytes=4096)
-        dec_scales = keep.tile([P, D], U8, name="dec_scales", align_bytes=4096)
+        dec_codes = tile([P, D], U32, "dec_codes")
+        dec_scales = tile([P, D], U8, "dec_scales")
         nc.vector.quantize_mx(out=dec_codes[:].bitcast(FP8X4), scales=dec_scales[:], in_=dec_bf[:])
 
-        for t, tag in ((2, "slot_c"), (3, "slot_b")):
-            plane = keep.tile([P, T], F32, name="keys%d" % t, tag=tag, align_bytes=4096)
-            nc.sync.dma_start(out=plane[:], in_=key_rows[t])
-            key_planes[t] = plane
+        key_rows = keys.rearrange("(p t) n -> t p n", t=PACK)
+        keys2 = tile([P, T], F32, "keys2", tag="scales")
+        nc.sync.dma_start(out=keys2[:], in_=key_rows[2])
+        keys3 = tile([P, T], F32, "keys3", tag="words")
+        nc.sync.dma_start(out=keys3[:], in_=key_rows[3])
 
-        picked = [keep.tile([P, I], F32, name="picked%d" % t, align_bytes=4096) for t in range(2)]
-        nc.vector.tensor_copy(picked[0][:], keys01[:, :T].indirect(offsets[:]))
-        nc.scalar.activation(picked[1][:], keys01[:, T:].indirect(offsets[:]), COPY)
+        picked0 = tile([P, I], F32, "picked0")
+        picked1 = tile([P, I], F32, "picked1")
+        nc.vector.tensor_copy(picked0[:], keys01[:, :T].indirect(offsets[:]))
+        nc.scalar.activation(picked1[:], keys01[:, T:].indirect(offsets[:]), COPY)
 
         def product(t, lo, hi):
             cols = slice(P * t, P * (t + 1))
@@ -90,47 +92,25 @@ def tile_attend_residualcache_pl_kernel(tc, code_words, code_scales, dec, keys, 
             )
             return acc
 
-        early = {(t, lo): product(t, lo, lo + I // 2) for lo in (0, I // 2) for t in range(2)}
-        decoded = {}
-        sums = {}
-        for t in range(2, PACK):
-            acc = product(t, 0, I)
-            sums[t] = acc
-            if t == 2:
-                halves = []
-                for lo, hi in PLANE2_CUTS:
-                    half = keep.tile([P, hi - lo], F32, name="picked2_%d" % lo, align_bytes=4096)
-                    cols = offsets[:, lo // 16 : hi // 16]
-                    nc.scalar.activation(half[:], key_planes[2][:].indirect(cols), COPY)
-                    halves.append(half)
-            if t < 3:
-                decoded[t] = acc
-            else:
-                b = keep.tile([P, SPLIT], F32, name="b%d" % t, tag="slot_c", align_bytes=4096)
-                nc.scalar.copy(out=b[:, :CHUNK], in_=acc[:, :CHUNK])
-                nc.scalar.copy(out=b[:, CHUNK:], in_=acc[:, CHUNK:SPLIT])
-                decoded[t] = b
+        early = {(t, 0): product(t, 0, HALF) for t in range(2)}
+        b3 = product(3, 0, I)
+        b3_copy = tile([P, SPLIT], F32, "b3_copy")
+        nc.scalar.copy(out=b3_copy[:], in_=b3[:, :SPLIT])
+        for t in range(2):
+            early[t, HALF] = product(t, HALF, I)
+        b2 = product(2, 0, I)
 
         y_rows = out_0.rearrange("(p t) i -> p t i", t=PACK)
-        y = keep.tile([P, PACK, I], F32, name="y", align_bytes=4096)
-        pieces = [(0, 128), (128, 256), (256, 320), (320, 448), (448, 512)]
-        y_bf = [
-            keep.tile([P, hi - lo, PACK], BF16, name="y_bf%d" % k, align_bytes=4096)
-            for k, (lo, hi) in enumerate(pieces)
-        ]
-        y_codes = keep.tile([P, I], U32, name="y_codes", align_bytes=4096)
-        y_scales = keep.tile([P, I], U8, name="y_scales", align_bytes=4096)
         word_rows = out_1[0].rearrange("p n t -> p (n t)").bitcast(I32)
-
-        def listed(lo, hi):
-            return offsets[:, lo // 16 : hi // 16]
+        y = tile([P, PACK, I], F32, "y")
+        pieces = [(0, 128), (128, 256), (256, 320), (320, 384), (384, 512)]
+        y_bf = [tile([P, hi - lo, PACK], BF16, "y_bf%d" % k) for k, (lo, hi) in enumerate(pieces)]
+        y_codes = tile([P, I], U32, "y_codes")
+        y_scales = tile([P, I], U8, "y_scales")
 
         def round_pair(copy, first, k):
             lo, hi = pieces[k]
-            copy(
-                out=y_bf[k][:, :, first : first + 2],
-                in_=y[:, first : first + 2, lo:hi].rearrange("p t i -> p i t"),
-            )
+            copy(out=y_bf[k][:, :, first : first + 2], in_=y[:, first : first + 2, lo:hi].rearrange("p t i -> p i t"))
 
         def quantise(k):
             lo, hi = pieces[k]
@@ -140,43 +120,47 @@ def tile_attend_residualcache_pl_kernel(tc, code_words, code_scales, dec, keys, 
                 in_=y_bf[k][:].rearrange("p i t -> p (i t)"),
             )
 
-        for lo in (0, I // 2):
-            cols = slice(lo, lo + I // 2)
-            for t in range(2):
-                nc.vector.tensor_tensor(y[:, t, cols], picked[t][:, cols], early[t, lo][:], SUB)
-        for t in range(2):
-            nc.sync.dma_start(out=y_rows[:, t, :], in_=y[:, t, :])
+        def store_plane(t, lo, hi):
+            nc.sync.dma_start(out=y_rows[:, t, lo:hi], in_=y[:, t, lo:hi])
+
+        def store_words(lo, hi):
+            nc.sync.dma_start(out=word_rows[:, lo:hi], in_=y_codes[:, lo:hi].bitcast(I32))
+
+        for lo in (0, HALF):
+            cols = slice(lo, lo + HALF)
+            for t, picked in enumerate((picked0, picked1)):
+                nc.vector.tensor_tensor(y[:, t, cols], picked[:, cols], early[t, lo][:], SUB)
+        store_plane(0, 0, I)
+        store_plane(1, 0, I)
         for k in range(len(pieces)):
             round_pair(nc.vector.tensor_copy, 0, k)
-        for half, (lo, hi) in zip(halves, PLANE2_CUTS):
-            nc.vector.tensor_tensor(y[:, 2, lo:hi], half[:], decoded[2][:, lo:hi], SUB)
-        nc.sync.dma_start(out=y_rows[:, 2, :], in_=y[:, 2, :])
 
-        last = key_planes[3]
-        picked3 = keep.tile([P, I - SPLIT], F32, name="picked3", align_bytes=4096)
-        nc.scalar.activation(picked3[:], last[:].indirect(listed(SPLIT, I)), COPY)
-        for lo, hi in ((0, CHUNK), (CHUNK, SPLIT)):
-            nc.vector.tensor_tensor(y[:, 3, lo:hi], last[:].indirect(listed(lo, hi)), decoded[3][:, lo:hi], SUB)
-            if lo == 0:
-                nc.sync.dma_start(out=y_rows[:, 3, :CHUNK], in_=y[:, 3, :CHUNK])
-        nc.vector.tensor_tensor(y[:, 3, SPLIT:], picked3[:], sums[3][:, SPLIT:], SUB)
-        nc.sync.dma_start(out=y_rows[:, 3, CHUNK:], in_=y[:, 3, CHUNK:])
+        for lo, hi in ((0, PLANE2_CUT), (PLANE2_CUT, I)):
+            picked2 = tile([P, hi - lo], F32, "picked2_%d" % lo)
+            nc.scalar.activation(picked2[:], keys2[:].indirect(listed(lo, hi)), COPY)
+            nc.vector.tensor_tensor(y[:, 2, lo:hi], picked2[:], b2[:, lo:hi], SUB)
+        store_plane(2, 0, I)
+
+        picked3 = tile([P, I - SPLIT], F32, "picked3")
+        nc.scalar.activation(picked3[:], keys3[:].indirect(listed(SPLIT, I)), COPY)
+        nc.vector.tensor_tensor(y[:, 3, :FIRST], keys3[:].indirect(listed(0, FIRST)), b3_copy[:, :FIRST], SUB)
+        store_plane(3, 0, FIRST)
+        nc.vector.tensor_tensor(y[:, 3, FIRST:SPLIT], keys3[:].indirect(listed(FIRST, SPLIT)), b3_copy[:, FIRST:], SUB)
+        nc.vector.tensor_tensor(y[:, 3, SPLIT:], picked3[:], b3[:, SPLIT:], SUB)
+        store_plane(3, FIRST, I)
         round_pair(nc.scalar.copy, 2, 0)
-        round_pair(nc.scalar.copy, 2, 1)
-        round_pair(nc.vector.tensor_copy, 2, 2)
-        quantise(0)
-        nc.sync.dma_start(out=word_rows[:, :128], in_=y_codes[:, :128].bitcast(I32))
-        round_pair(nc.vector.tensor_copy, 2, 3)
+        round_pair(nc.scalar.copy, 2, 2)
         round_pair(nc.scalar.copy, 2, 4)
-        quantise(2)
+        round_pair(nc.vector.tensor_copy, 2, 1)
+        quantise(0)
+        store_words(0, 128)
+        round_pair(nc.vector.tensor_copy, 2, 3)
         quantise(1)
-        nc.sync.dma_start(out=word_rows[:, 128:320], in_=y_codes[:, 128:320].bitcast(I32))
+        quantise(2)
+        store_words(128, 320)
         quantise(3)
         quantise(4)
-        nc.sync.dma_start(out=word_rows[:, 320:], in_=y_codes[:, 320:].bitcast(I32))
+        store_words(320, 512)
         for r in range(4):
             queue = nc.scalar if r % 2 == 0 else nc.sync
-            queue.dma_start(
-                out=out_2[0, r:16:4, :].bitcast(I32),
-                in_=y_scales[r:P:32, :].bitcast(I32),
-            )
+            queue.dma_start(out=out_2[0, r:16:4, :].bitcast(I32), in_=y_scales[r:P:32, :].bitcast(I32))

@@ -46,7 +46,7 @@ def tile_attend_residualcache_pl_kernel(tc, code_words, code_scales, dec, keys, 
         nc.vector.memset(scales[:].bitcast(I32), 0)
         nc.sync.dma_start(out=words[:].bitcast(I32), in_=code_words[0].rearrange("p n t -> p (n t)").bitcast(I32))
         nc.sync.dma_start(offsets[:], offs)
-        nc.sync.dma_start(out=scales[0:P:8, :].bitcast(I32), in_=code_scales[0].bitcast(I32))
+        nc.sync.dma_start(out=scales[0:P:8, :].bitcast(I32), in_=code_scales[0].bitcast(I32), max_dma_last_dim=T // 2)
         nc.sync.dma_start(out=dec_raw[:], in_=dec.rearrange("(p j) d -> p (j d)", j=PACK))
         nc.sync.dma_start(out=keys01[:], in_=keys.rearrange("(p u t) n -> u p (t n)", u=2, t=2)[0])
 
@@ -139,7 +139,7 @@ def tile_attend_residualcache_pl_kernel(tc, code_words, code_scales, dec, keys, 
             picked2 = tile([P, hi - lo], F32, "picked2_%d" % lo)
             nc.scalar.activation(picked2[:], keys2[:].indirect(listed(lo, hi)), COPY)
             nc.vector.tensor_tensor(y[:, 2, lo:hi], picked2[:], b2[:, lo:hi], SUB)
-        store_plane(2, 0, I)
+            store_plane(2, lo, hi)
 
         picked3 = tile([P, I - SPLIT], F32, "picked3")
         nc.scalar.activation(picked3[:], keys3[:].indirect(listed(SPLIT, I)), COPY)

@@ -18,11 +18,11 @@ COPY = mybir.ActivationFunctionType.Copy
 P = 128
 PACK = 4
 ALIGN = 4096
+WORK_ALIGN = 256
 HALF = I // 2
 SCALAR_M = 80
 FIRST = 128
 SPLIT = 320
-PLANE2_CUT = 384
 
 
 def tile_attend_residualcache_pl_kernel(tc, code_words, code_scales, dec, keys, offs, out_0, out_1, out_2):
@@ -33,6 +33,9 @@ def tile_attend_residualcache_pl_kernel(tc, code_words, code_scales, dec, keys, 
 
         def tile(shape, dtype, name, tag=None):
             return keep.tile(shape, dtype, name=name, tag=tag or name, align_bytes=ALIGN)
+
+        def work(shape, dtype, name):
+            return keep.tile(shape, dtype, name=name, align_bytes=WORK_ALIGN)
 
         offsets = tile([P, I // 16], U16, "offsets")
         words = tile([P, T], U32, "words")
@@ -73,9 +76,10 @@ def tile_attend_residualcache_pl_kernel(tc, code_words, code_scales, dec, keys, 
         keys3 = tile([P, T], F32, "keys3", tag="words")
         nc.sync.dma_start(out=keys3[:], in_=key_rows[3])
 
-        picked0 = tile([P, I], F32, "picked0")
-        picked1 = tile([P, I], F32, "picked1")
-        nc.vector.tensor_copy(picked0[:], keys01[:, :T].indirect(offsets[:]))
+        picked0 = [work([P, HALF], F32, "picked0_%d" % lo) for lo in (0, HALF)]
+        picked1 = work([P, I], F32, "picked1")
+        for k, lo in enumerate((0, HALF)):
+            nc.vector.tensor_copy(picked0[k][:], keys01[:, :T].indirect(listed(lo, lo + HALF)))
         nc.scalar.activation(picked1[:], keys01[:, T:].indirect(offsets[:]), COPY)
 
         def product(t, lo, hi):
@@ -92,12 +96,12 @@ def tile_attend_residualcache_pl_kernel(tc, code_words, code_scales, dec, keys, 
             )
             return acc
 
-        early = {(t, 0): product(t, 0, HALF) for t in range(2)}
+        b0 = product(0, 0, I)
+        b1_low = product(1, 0, HALF)
         b3 = product(3, 0, I)
-        b3_copy = tile([P, SPLIT], F32, "b3_copy")
+        b3_copy = work([P, SPLIT], F32, "b3_copy")
         nc.scalar.copy(out=b3_copy[:], in_=b3[:, :SPLIT])
-        for t in range(2):
-            early[t, HALF] = product(t, HALF, I)
+        b1_high = product(1, HALF, I)
         b2 = product(2, 0, I)
 
         y_rows = out_0.rearrange("(p t) i -> p t i", t=PACK)
@@ -108,9 +112,9 @@ def tile_attend_residualcache_pl_kernel(tc, code_words, code_scales, dec, keys, 
         y_codes = tile([P, I], U32, "y_codes")
         y_scales = tile([P, I], U8, "y_scales")
 
-        def round_pair(copy, first, k):
+        def round_planes(copy, first, last, k):
             lo, hi = pieces[k]
-            copy(out=y_bf[k][:, :, first : first + 2], in_=y[:, first : first + 2, lo:hi].rearrange("p t i -> p i t"))
+            copy(out=y_bf[k][:, :, first:last], in_=y[:, first:last, lo:hi].rearrange("p t i -> p i t"))
 
         def quantise(k):
             lo, hi = pieces[k]
@@ -126,35 +130,44 @@ def tile_attend_residualcache_pl_kernel(tc, code_words, code_scales, dec, keys, 
         def store_words(lo, hi):
             nc.sync.dma_start(out=word_rows[:, lo:hi], in_=y_codes[:, lo:hi].bitcast(I32))
 
-        for lo in (0, HALF):
-            cols = slice(lo, lo + HALF)
-            for t, picked in enumerate((picked0, picked1)):
-                nc.vector.tensor_tensor(y[:, t, cols], picked[:, cols], early[t, lo][:], SUB)
+        for k, lo in enumerate((0, HALF)):
+            nc.vector.tensor_tensor(y[:, 0, lo : lo + HALF], picked0[k][:], b0[:, lo : lo + HALF], SUB)
         store_plane(0, 0, I)
+        nc.vector.tensor_tensor(y[:, 1, :HALF], picked1[:, :HALF], b1_low[:], SUB)
+        nc.vector.tensor_tensor(y[:, 1, HALF:], picked1[:, HALF:], b1_high[:], SUB)
         store_plane(1, 0, I)
-        for k in range(len(pieces)):
-            round_pair(nc.vector.tensor_copy, 0, k)
 
-        for lo, hi in ((0, PLANE2_CUT), (PLANE2_CUT, I)):
-            picked2 = tile([P, hi - lo], F32, "picked2_%d" % lo)
-            nc.scalar.activation(picked2[:], keys2[:].indirect(listed(lo, hi)), COPY)
-            nc.vector.tensor_tensor(y[:, 2, lo:hi], picked2[:], b2[:, lo:hi], SUB)
-            store_plane(2, lo, hi)
+        low2 = [work([P, FIRST], F32, "low2_%d" % k) for k in range(2)]
+        high2 = work([P, HALF], F32, "high2")
+        nc.scalar.activation(high2[:], keys2[:].indirect(listed(HALF, I)), COPY)
+        for k in range(2):
+            nc.vector.tensor_copy(low2[k][:], keys2[:].indirect(listed(k * FIRST, (k + 1) * FIRST)))
+        for k in range(2):
+            cols = slice(k * FIRST, (k + 1) * FIRST)
+            nc.vector.tensor_tensor(y[:, 2, cols], low2[k][:], b2[:, cols], SUB)
+        store_plane(2, 0, HALF)
+        nc.vector.tensor_tensor(y[:, 2, HALF:], high2[:], b2[:, HALF:], SUB)
+        store_plane(2, HALF, I)
+        round_planes(nc.scalar.copy, 0, 3, 0)
+        round_planes(nc.vector.tensor_copy, 0, 3, 1)
+        round_planes(nc.scalar.copy, 0, 3, 2)
+        round_planes(nc.vector.tensor_copy, 0, 3, 3)
+        round_planes(nc.vector.tensor_copy, 0, 3, 4)
 
-        picked3 = tile([P, I - SPLIT], F32, "picked3")
+        picked3 = work([P, I - SPLIT], F32, "picked3")
         nc.scalar.activation(picked3[:], keys3[:].indirect(listed(SPLIT, I)), COPY)
         nc.vector.tensor_tensor(y[:, 3, :FIRST], keys3[:].indirect(listed(0, FIRST)), b3_copy[:, :FIRST], SUB)
         store_plane(3, 0, FIRST)
         nc.vector.tensor_tensor(y[:, 3, FIRST:SPLIT], keys3[:].indirect(listed(FIRST, SPLIT)), b3_copy[:, FIRST:], SUB)
         nc.vector.tensor_tensor(y[:, 3, SPLIT:], picked3[:], b3[:, SPLIT:], SUB)
         store_plane(3, FIRST, I)
-        round_pair(nc.scalar.copy, 2, 0)
-        round_pair(nc.scalar.copy, 2, 2)
-        round_pair(nc.scalar.copy, 2, 4)
-        round_pair(nc.vector.tensor_copy, 2, 1)
+        round_planes(nc.scalar.copy, 3, 4, 0)
+        round_planes(nc.scalar.copy, 3, 4, 2)
+        round_planes(nc.scalar.copy, 3, 4, 4)
+        round_planes(nc.vector.tensor_copy, 3, 4, 1)
         quantise(0)
         store_words(0, 128)
-        round_pair(nc.vector.tensor_copy, 2, 3)
+        round_planes(nc.vector.tensor_copy, 3, 4, 3)
         quantise(1)
         quantise(2)
         store_words(128, 320)

@@ -137,22 +137,23 @@ def tile_attend_residualcache_pl_kernel(tc, code_words, code_scales, dec, keys, 
         nc.vector.tensor_tensor(y[:, 1, HALF:], picked1[:, HALF:], b1_high[:], SUB)
         store_plane(1, 0, I)
 
-        low2 = [work([P, FIRST], F32, "low2_%d" % k) for k in range(2)]
-        high2 = work([P, HALF], F32, "high2")
-        nc.scalar.activation(high2[:], keys2[:].indirect(listed(HALF, I)), COPY)
-        for k in range(2):
-            nc.vector.tensor_copy(low2[k][:], keys2[:].indirect(listed(k * FIRST, (k + 1) * FIRST)))
-        for k in range(2):
-            cols = slice(k * FIRST, (k + 1) * FIRST)
-            nc.vector.tensor_tensor(y[:, 2, cols], low2[k][:], b2[:, cols], SUB)
-        store_plane(2, 0, HALF)
-        nc.vector.tensor_tensor(y[:, 2, HALF:], high2[:], b2[:, HALF:], SUB)
-        store_plane(2, HALF, I)
-        round_planes(nc.scalar.copy, 0, 3, 0)
-        round_planes(nc.vector.tensor_copy, 0, 3, 1)
-        round_planes(nc.scalar.copy, 0, 3, 2)
-        round_planes(nc.vector.tensor_copy, 0, 3, 3)
-        round_planes(nc.vector.tensor_copy, 0, 3, 4)
+        for k in (0, 2, 4):
+            round_planes(nc.vector.tensor_copy, 0, 2, k)
+
+        parts2 = {}
+        for lo, hi in ((128, 384), (384, 512), (0, 128)):
+            parts2[lo] = work([P, hi - lo], F32, "picked2_%d" % lo)
+            if lo == 384:
+                nc.vector.tensor_copy(parts2[lo][:], keys2[:].indirect(listed(lo, hi)))
+            else:
+                nc.scalar.activation(parts2[lo][:], keys2[:].indirect(listed(lo, hi)), COPY)
+        for lo, hi in ((128, 384), (384, 512)):
+            nc.vector.tensor_tensor(y[:, 2, lo:hi], parts2[lo][:], b2[:, lo:hi], SUB)
+        store_plane(2, 128, I)
+        nc.vector.tensor_tensor(y[:, 2, :128], parts2[0][:], b2[:, :128], SUB)
+        store_plane(2, 0, 128)
+        for k in (1, 3):
+            round_planes(nc.vector.tensor_copy, 0, 3, k)
 
         picked3 = work([P, I - SPLIT], F32, "picked3")
         nc.scalar.activation(picked3[:], keys3[:].indirect(listed(SPLIT, I)), COPY)
@@ -161,9 +162,9 @@ def tile_attend_residualcache_pl_kernel(tc, code_words, code_scales, dec, keys, 
         nc.vector.tensor_tensor(y[:, 3, FIRST:SPLIT], keys3[:].indirect(listed(FIRST, SPLIT)), b3_copy[:, FIRST:], SUB)
         nc.vector.tensor_tensor(y[:, 3, SPLIT:], picked3[:], b3[:, SPLIT:], SUB)
         store_plane(3, FIRST, I)
-        round_planes(nc.scalar.copy, 3, 4, 0)
-        round_planes(nc.scalar.copy, 3, 4, 2)
-        round_planes(nc.scalar.copy, 3, 4, 4)
+        round_planes(nc.scalar.copy, 2, 4, 0)
+        round_planes(nc.scalar.copy, 2, 4, 2)
+        round_planes(nc.scalar.copy, 2, 4, 4)
         round_planes(nc.vector.tensor_copy, 3, 4, 1)
         quantise(0)
         store_words(0, 128)

from contextlib import ExitStack

import concourse.mybir as mybir

C, T, I, D = 512, 2048, 512, 512
FLOPS = 2 * C * D * I

F32 = mybir.dt.float32
BF16 = mybir.dt.bfloat16
I32 = mybir.dt.int32
U32 = mybir.dt.uint32
U16 = mybir.dt.uint16
U8 = mybir.dt.uint8
FP8X4 = mybir.dt.float8_e4m3fn_x4
SUB = mybir.AluOpType.subtract
COPY = mybir.ActivationFunctionType.Copy

P = 128
PACK = 4
ALIGN = 4096
WORK_ALIGN = 256
HALF = I // 2
SCALAR_M = 80
FIRST = 128
SPLIT = 320


def tile_attend_residualcache_pl_kernel(tc, code_words, code_scales, dec, keys, offs, out_0, out_1, out_2):
    nc = tc.nc
    with ExitStack() as ctx:
        keep = ctx.enter_context(tc.tile_pool(name="keep", bufs=1))
        psum = ctx.enter_context(tc.psum_pool(name="psum", bufs=1))

        def tile(shape, dtype, name, tag=None):
            return keep.tile(shape, dtype, name=name, tag=tag or name, align_bytes=ALIGN)

        def work(shape, dtype, name):
            return keep.tile(shape, dtype, name=name, align_bytes=WORK_ALIGN)

        offsets = tile([P, I // 16], U16, "offsets")
        words = tile([P, T], U32, "words")
        scales = tile([P, T], U8, "scales")
        dec_raw = tile([P, PACK * D], F32, "dec_raw")
        keys01 = tile([P, 2 * T], F32, "keys01")

        def listed(lo, hi):
            return offsets[:, lo // 16 : hi // 16]

        nc.vector.memset(scales[:].bitcast(I32), 0)
        nc.sync.dma_start(out=words[:].bitcast(I32), in_=code_words[0].rearrange("p n t -> p (n t)").bitcast(I32))
        nc.sync.dma_start(offsets[:], offs)
        nc.sync.dma_start(out=scales[0:P:8, :].bitcast(I32), in_=code_scales[0].bitcast(I32), max_dma_last_dim=T // 2)
        nc.sync.dma_start(out=dec_raw[:], in_=dec.rearrange("(p j) d -> p (j d)", j=PACK))
        nc.sync.dma_start(out=keys01[:], in_=keys.rearrange("(p u t) n -> u p (t n)", u=2, t=2)[0])

        scales_s = tile([P, I], U8, "scales_s")
        nc.vector.tensor_copy(scales_s[:], scales[:].indirect(offsets[:]))
        scales_g = tile([P, I], U8, "scales_g")
        nc.vector.tensor_copy(out=scales_g[:].bitcast(I32), in_=scales_s[:].bitcast(I32))
        for r in range(1, 4):
            nc.sync.dma_start(out=scales_g[r:P:32, :].bitcast(I32), in_=scales_s[8 * r : P : 32, :].bitcast(I32))
        words_g = tile([P, I], U32, "words_g")
        nc.vector.tensor_copy(words_g[:], words[:].indirect(offsets[:]))
        dec_bf = tile([P, D * PACK], BF16, "dec_bf")
        dealt = dec_bf[:].rearrange("p (t m j) -> p m t j", t=PACK, j=PACK)
        source = dec_raw[:].rearrange("p (j m t) -> p m t j", j=PACK, t=PACK)
        nc.scalar.copy(out=dealt[:, :SCALAR_M], in_=source[:, :SCALAR_M])
        nc.vector.tensor_copy(out=dealt[:, SCALAR_M:], in_=source[:, SCALAR_M:])
        dec_codes = tile([P, D], U32, "dec_codes")
        dec_scales = tile([P, D], U8, "dec_scales")
        nc.vector.quantize_mx(out=dec_codes[:].bitcast(FP8X4), scales=dec_scales[:], in_=dec_bf[:])

        key_rows = keys.rearrange("(p t) n -> t p n", t=PACK)
        keys2 = tile([P, T], F32, "keys2", tag="scales")
        nc.sync.dma_start(out=keys2[:], in_=key_rows[2])
        keys3 = tile([P, T], F32, "keys3", tag="words")
        nc.sync.dma_start(out=keys3[:], in_=key_rows[3])

        picked0 = [work([P, HALF], F32, "picked0_%d" % lo) for lo in (0, HALF)]
        picked1 = work([P, I], F32, "picked1")
        for k, lo in enumerate((0, HALF)):
            nc.vector.tensor_copy(picked0[k][:], keys01[:, :T].indirect(listed(lo, lo + HALF)))
        nc.scalar.activation(picked1[:], keys01[:, T:].indirect(offsets[:]), COPY)

        def product(t, lo, hi):
            cols = slice(P * t, P * (t + 1))
            acc = psum.tile([P, hi - lo], F32, name="acc%d_%d" % (t, lo))
            nc.tensor.matmul_mx(
                out=acc[:],
                lhsT=dec_codes[:, cols].bitcast(FP8X4),
                lhsT_scale=dec_scales[:, cols],
                rhs=words_g[:, lo:hi].bitcast(FP8X4),
                rhs_scale=scales_g[:, lo:hi],
                start=True,
                stop=True,
            )
            return acc

        b0 = product(0, 0, I)
        b1_low = product(1, 0, HALF)
        b3 = product(3, 0, I)
        b3_copy = work([P, SPLIT], F32, "b3_copy")
        nc.scalar.copy(out=b3_copy[:], in_=b3[:, :SPLIT])
        b1_high = product(1, HALF, I)
        b2 = product(2, 0, I)

        y_rows = out_0.rearrange("(p t) i -> p t i", t=PACK)
        word_rows = out_1[0].rearrange("p n t -> p (n t)").bitcast(I32)
        y = tile([P, PACK, I], F32, "y")
        pieces = [(0, 128), (128, 256), (256, 320), (320, 384), (384, 512)]
        y_bf = [tile([P, hi - lo, PACK], BF16, "y_bf%d" % k) for k, (lo, hi) in enumerate(pieces)]
        y_codes = tile([P, I], U32, "y_codes")
        y_scales = tile([P, I], U8, "y_scales")

        def round_planes(copy, first, last, k):
            lo, hi = pieces[k]
            copy(out=y_bf[k][:, :, first:last], in_=y[:, first:last, lo:hi].rearrange("p t i -> p i t"))

        def quantise(k):
            lo, hi = pieces[k]
            nc.vector.quantize_mx(
                out=y_codes[:, lo:hi].bitcast(FP8X4),
                scales=y_scales[:, lo:hi],
                in_=y_bf[k][:].rearrange("p i t -> p (i t)"),
            )

        def store_plane(t, lo, hi):
            nc.sync.dma_start(out=y_rows[:, t, lo:hi], in_=y[:, t, lo:hi])

        def store_words(lo, hi):
            nc.sync.dma_start(out=word_rows[:, lo:hi], in_=y_codes[:, lo:hi].bitcast(I32))

        for k, lo in enumerate((0, HALF)):
            nc.vector.tensor_tensor(y[:, 0, lo : lo + HALF], picked0[k][:], b0[:, lo : lo + HALF], SUB)
        store_plane(0, 0, I)
        nc.vector.tensor_tensor(y[:, 1, :HALF], picked1[:, :HALF], b1_low[:], SUB)
        nc.vector.tensor_tensor(y[:, 1, HALF:], picked1[:, HALF:], b1_high[:], SUB)
        store_plane(1, 0, I)

        for k in (0, 2, 4):
            round_planes(nc.vector.tensor_copy, 0, 2, k)

        parts2 = {}
        for lo, hi in ((128, 384), (384, 512), (0, 128)):
            parts2[lo] = work([P, hi - lo], F32, "picked2_%d" % lo)
            if lo == 384:
                nc.vector.tensor_copy(parts2[lo][:], keys2[:].indirect(listed(lo, hi)))
            else:
                nc.scalar.activation(parts2[lo][:], keys2[:].indirect(listed(lo, hi)), COPY)
        for lo, hi in ((128, 384), (384, 512)):
            nc.vector.tensor_tensor(y[:, 2, lo:hi], parts2[lo][:], b2[:, lo:hi], SUB)
        store_plane(2, 128, I)
        nc.vector.tensor_tensor(y[:, 2, :128], parts2[0][:], b2[:, :128], SUB)
        store_plane(2, 0, 128)
        for k in (1, 3):
            round_planes(nc.vector.tensor_copy, 0, 3, k)

        picked3 = work([P, I - SPLIT], F32, "picked3")
        nc.scalar.activation(picked3[:], keys3[:].indirect(listed(SPLIT, I)), COPY)
        nc.vector.tensor_tensor(y[:, 3, :FIRST], keys3[:].indirect(listed(0, FIRST)), b3_copy[:, :FIRST], SUB)
        store_plane(3, 0, FIRST)
        nc.vector.tensor_tensor(y[:, 3, FIRST:SPLIT], keys3[:].indirect(listed(FIRST, SPLIT)), b3_copy[:, FIRST:], SUB)
        nc.vector.tensor_tensor(y[:, 3, SPLIT:], picked3[:], b3[:, SPLIT:], SUB)
        store_plane(3, FIRST, I)
        round_planes(nc.scalar.copy, 2, 4, 0)
        round_planes(nc.scalar.copy, 2, 4, 2)
        round_planes(nc.scalar.copy, 2, 4, 4)
        round_planes(nc.vector.tensor_copy, 3, 4, 1)
        quantise(0)
        store_words(0, 128)
        round_planes(nc.vector.tensor_copy, 3, 4, 3)
        quantise(1)
        quantise(2)
        store_words(128, 320)
        quantise(3)
        quantise(4)
        store_words(320, 512)
        for r in range(4):
            queue = nc.scalar if r % 2 == 0 else nc.sync
            queue.dma_start(out=out_2[0, r:16:4, :].bitcast(I32), in_=y_scales[r:P:32, :].bitcast(I32))
